import numpy as np
import ml_dtypes


def mxq(x, axis, fmt="e4m3"):
    dtype, down = {"e4m3": (ml_dtypes.float8_e4m3fn, 7), "e5m2": (ml_dtypes.float8_e5m2, 14)}[fmt]
    v = np.moveaxis(np.asarray(x, np.float32).astype(ml_dtypes.bfloat16).astype(np.float64), axis, -1)
    blocks = v.reshape(v.shape[:-1] + (-1, 32))
    amax = np.abs(blocks).max(-1, keepdims=True)
    byte = np.maximum(np.where(amax > 0, np.frexp(amax)[1] - 1 + 127, 0) - down, 1)
    scale = np.exp2(byte - 127.0)
    codes = (blocks / scale).astype(np.float32).astype(dtype).astype(np.float64)
    return np.moveaxis((codes * scale).reshape(v.shape), -1, axis)


WIDE = False


def mx_kscale(k):
    if not WIDE:
        return np.ones(k)
    levels = np.array([10, -10, 5, -5, 0])
    if k % 512:
        return np.exp2(np.random.permutation(np.resize(levels, k // 32))).repeat(32)
    a = np.empty((k // 512, 16))
    for p in range(k // 512):
        a[p, :8] = np.random.permutation(np.resize(levels, 8))
        for g in range(8):
            far = levels[np.abs(levels - a[p, g]) >= 10]
            a[p, g + 8] = far[np.random.randint(len(far))]
    return np.exp2(a.ravel()).repeat(32)


def f64(x):
    return np.asarray(x).astype(np.float64)


def striped(idx):
    return np.tile(idx.reshape(-1, 16).T, (8, 1)).astype(np.uint16)


def unstriped(offs):
    return offs[:16].T.reshape(-1).astype(np.int64)


def striped8(idx):
    return np.concatenate([x.reshape(-1, 16).T for x in idx]).astype(np.uint16)


def runs(offs, k):
    lists = np.stack([offs[16 * r : 16 * r + 16].T.reshape(-1) for r in range(8)]).astype(np.int64)
    return lists[np.arange(k) % 512 // 64]


def pack_weight(w):
    k, n = w.shape
    w = f64(np.asarray(w, np.float32).astype(ml_dtypes.bfloat16)).reshape(k // 32, 32, n)
    amax = np.abs(w).max(1)
    byte = np.clip(np.where(amax > 0, np.frexp(amax)[1] - 1 + 127 - 7, 1), 1, 254)
    scaled = (w * np.exp2(127.0 - byte)[:, None, :]).reshape(k, n).astype(np.float32)
    words = np.ascontiguousarray(scaled.reshape(k // 512, 128, 4, n).transpose(0, 1, 3, 2)).astype(ml_dtypes.float8_e4m3fn).view(np.uint8)
    return words, np.ascontiguousarray(byte.astype(np.uint8).reshape(k // 512, 16, n))


def unpack_weight(words, scales):
    g, p, n, _ = words.shape
    vals = np.ascontiguousarray(words).view(ml_dtypes.float8_e4m3fn).astype(np.float64) * np.repeat(np.exp2(scales.astype(np.float64) - 127.0), 8, axis=1)[..., None]
    return vals.transpose(0, 1, 3, 2).reshape(g * 512, n)


def sigmoid(v):
    return 1.0 / (1.0 + np.exp(-np.maximum(v, -700.0)))


K, T, S, H, C = 512, 2048, 512, 512, 512


def setup_inputs():
    n = np.random.standard_normal
    s = mx_kscale(K)[:, None]
    packed_xT = pack_weight(n((K, T)) * s)
    return {
        "x_words": packed_xT[0],
        "x_scales": packed_xT[1],
        "w1": (n((K, H)) / np.sqrt(K) / s).astype(np.float32),
        "w2": (n((K, H)) / np.sqrt(K) / s).astype(np.float32),
        "gs": (np.random.uniform(0.5, 1.5, (K, 1)) / s).astype(np.float32),
        "offs": striped(np.random.permutation(T)[:S]),
        "two": striped(np.random.permutation(T)[:S]),
        "n1": striped8(np.stack([np.random.permutation(S) for _ in range(8)])),
        "n2": striped8(np.stack([np.random.permutation(S) for _ in range(8)])),
        "cand": striped(np.random.permutation(T)[:C]),
        "n3": striped8(np.stack([np.random.permutation(S) for _ in range(8)])),
    }


def reference(x_words, x_scales, w1, w2, gs, offs, two, n1, n2, cand, n3):
    x_cand = unpack_weight(x_words, x_scales)[:, unstriped(cand)]
    xq = unpack_weight(x_words, x_scales)[:, unstriped(offs)]
    y = mxq(f64(w1), 0, "e4m3").T @ xq
    x_two = unpack_weight(x_words, x_scales)[:, unstriped(two)]
    d = mxq(f64(w2), 0, "e4m3").T @ x_two
    z = f64(gs) * (y * (sigmoid(d[np.arange(H)[:, None], runs(n2, H)])) - (0.5 * (y[np.arange(H)[:, None], runs(n1, H)])))
    s = 0.0625 * ((x_cand.T @ mxq(z, 0, "e4m3")))
    st = s - (s[np.arange(C)[:, None], runs(n3, C)])
    return st - (0.5 * (st[np.arange(C)[:, None], runs(n3, C)]))

@@ -1,0 +1,161 @@
+from contextlib import ExitStack
+
+import concourse.mybir as mybir
+
+K, T, S, H, C = 512, 2048, 512, 512, 512
+FLOPS = 3 * 2 * 512 * 512 * 512
+
+F32 = mybir.dt.float32
+BF16 = mybir.dt.bfloat16
+I32 = mybir.dt.int32
+U32 = mybir.dt.uint32
+U16 = mybir.dt.uint16
+U8 = mybir.dt.uint8
+FP8X4 = mybir.dt.float8_e4m3fn_x4
+ALU = mybir.AluOpType
+ACT = mybir.ActivationFunctionType
+
+P = 128
+PACK = 4
+WIN = 2 * S
+CHUNKS = 2
+
+
+def tile_picked_twcgatebtwice_none_p_kernel(tc, x_words, x_scales, w1, w2, gs, offs, two, n1, n2, cand, n3, out):
+    nc = tc.nc
+    with ExitStack() as ctx:
+        keep = ctx.enter_context(tc.tile_pool(name="keep", bufs=1))
+        psum = ctx.enter_context(tc.psum_pool(name="psum", bufs=1))
+
+        def load_list(src, name):
+            tile = keep.tile([P, S // 16], U16, name=name)
+            nc.sync.dma_start(tile[:], src)
+            return tile
+
+        xs = keep.tile([P, T], U8, name="xs", align_bytes=64)
+        warm = keep.tile([P, 2], F32, name="warm")
+        nc.gpsimd.memset(warm[:, 0:1], 0.0)
+        nc.scalar.activation(warm[:, 1:2], warm[:, 0:1], ACT.Sigmoid)
+
+        l_two = load_list(two, "l_two")
+        for q in range(4):
+            nc.sync.dma_start(xs[32 * q : 32 * q + 32, :].bitcast(I32),
+                              x_scales[0, 4 * q : 4 * q + 4, :].bitcast(I32).partition_broadcast(8))
+        l_offs = load_list(offs, "l_offs")
+        cw = H // CHUNKS
+
+        def load_w(w, name):
+            rows = w.rearrange("(p j) c -> p j c", j=PACK)
+            raws = []
+            for h in range(CHUNKS):
+                raw = keep.tile([P, PACK, cw], F32, name=f"{name}_raw{h}")
+                nc.sync.dma_start(raw[:], rows[:, :, h * cw : (h + 1) * cw])
+                raws.append(raw)
+            return raws
+
+        w2_raw = load_w(w2, "w2")
+        xw = keep.tile([P, T], I32, name="xw", align_bytes=64)
+        nc.sync.dma_start(xw[:], x_words[0].rearrange("p n r -> p (n r)").bitcast(I32))
+        l_cand = load_list(cand, "l_cand")
+        w1_raw = load_w(w1, "w1")
+        gain = keep.tile([P, PACK], F32, name="gain")
+        nc.sync.dma_start(gain[:], gs.rearrange("(p t) o -> p (t o)", t=PACK))
+        l_n2 = load_list(n2, "l_n2")
+        l_n1 = load_list(n1, "l_n1")
+        l_n3 = load_list(n3, "l_n3")
+
+        def gather_bytes(lst, name):
+            g = keep.tile([P, S], U8, name=name, align_bytes=64)
+            nc.vector.tensor_copy(g[:], xs[:].indirect(lst[:]))
+            return g
+
+        def gather_words(lst, name):
+            g = keep.tile([P, S], U32, name=name, align_bytes=64)
+            nc.vector.tensor_copy(g[:], xw[:].bitcast(U32).indirect(lst[:]))
+            return g
+
+        def weave_w(raws, name, on_scalar):
+            grouped = keep.tile([P, PACK, P, PACK], BF16, name=name, align_bytes=64)
+            mw = cw // PACK
+            for h in range(CHUNKS):
+                dst = grouped[:, :, h * mw : (h + 1) * mw, :].rearrange("p t m j -> p m t j")
+                src = raws[h][:].rearrange("p j (m t) -> p m t j", t=PACK)
+                if on_scalar:
+                    nc.scalar.copy(dst, src)
+                else:
+                    nc.gpsimd.tensor_scalar(dst, src, 1.0, 0.0, ALU.mult, ALU.add)
+            return grouped
+
+        def quantize(src, name):
+            codes = keep.tile([P, S], U32, name=name + "_codes", align_bytes=64)
+            scales = keep.tile([P, S], U8, name=name + "_scales", align_bytes=64)
+            nc.vector.quantize_mx(out=codes[:].bitcast(FP8X4), scales=scales[:], in_=src)
+            return codes, scales
+
+        def product(lhs, lhs_s, rhs, rhs_s, t, tag):
+            bank = psum.tile([P, S], F32, name=tag, tag=tag)
+            cols = slice(t * P, (t + 1) * P)
+            nc.tensor.matmul_mx(out=bank[:], lhsT=lhs[:, cols].bitcast(FP8X4), lhsT_scale=lhs_s[:, cols],
+                                rhs=rhs[:].bitcast(FP8X4), rhs_scale=rhs_s[:], start=True, stop=True)
+            return bank
+
+        two_b = gather_bytes(l_two, "two_b")
+        offs_b = gather_bytes(l_offs, "offs_b")
+        cand_b0 = gather_bytes(l_cand, "cand_b0")
+        w2_g = weave_w(w2_raw, "w2_g", True)
+        w2_c, w2_s = quantize(w2_g[:].rearrange("p t m j -> p (t m j)"), "w2")
+        two_w = gather_words(l_two, "two_w")
+        offs_w = gather_words(l_offs, "offs_w")
+        cand_w = keep.tile([P, S], U32, name="cand_w", align_bytes=64)
+        nc.vector.tensor_copy(cand_w[:].rearrange("p (t s) -> p s t", t=PACK), xw[:].bitcast(U32).indirect(l_cand[:]))
+        cand_b = keep.tile([P, S], U8, name="cand_b", align_bytes=64)
+        nc.vector.tensor_copy(cand_b[:].rearrange("p (t s) -> p t s", t=PACK), cand_b0[:].rearrange("p (s t) -> p t s", t=PACK))
+        w1_g = weave_w(w1_raw, "w1_g", False)
+        w1_c, w1_s = quantize(w1_g[:].rearrange("p t m j -> p (t m j)"), "w1")
+        half_gain = keep.tile([P, PACK], F32, name="half_gain")
+        nc.gpsimd.tensor_scalar(half_gain[:], gain[:], -0.5, 0.0, ALU.mult, ALU.add)
+
+        d_bank = [product(w2_c, w2_s, two_w, two_b, t, f"a{t}") for t in range(PACK)]
+        y_bank = [product(w1_c, w1_s, offs_w, offs_b, t, f"b{t}") for t in range(PACK)]
+
+        sig = []
+        for t in range(PACK):
+            d_win = keep.tile([P, WIN], F32, name=f"d_win{t}")
+            nc.scalar.copy(d_win[:, 0:S], d_bank[t][:])
+            sg = keep.tile([P, S], F32, name=f"sig{t}")
+            nc.scalar.activation(sg[:], d_win[:].indirect(l_n2[:]), ACT.Sigmoid)
+            sig.append(sg)
+
+        z4 = keep.tile([P, PACK, S], F32, name="z4")
+        for t in range(PACK):
+            u_win = keep.tile([P, WIN], F32, name=f"u_win{t}")
+            nc.scalar.activation(u_win[:, 0:S], y_bank[t][:], ACT.Copy, scale=half_gain[:, t : t + 1])
+            a = keep.tile([P, S], F32, name=f"gated{t}")
+            nc.vector.scalar_tensor_tensor(a[:], y_bank[t][:], gain[:, t : t + 1], sig[t][:], ALU.mult, ALU.mult)
+            nc.vector.tensor_tensor(z4[:, t, :], u_win[:].indirect(l_n1[:]), a[:], ALU.add)
+
+        z_g = keep.tile([P, S, PACK], BF16, name="z_g", align_bytes=64)
+        split = 352
+        nc.vector.tensor_copy(z_g[:, 0:split, :].rearrange("p (c i) t -> p c t i", i=4),
+                              z4[:, :, 0:split].rearrange("p t (c i) -> p c t i", i=4))
+        nc.scalar.copy(z_g[:, split:S, :].rearrange("p (c i) t -> p c t i", i=4),
+                       z4[:, :, split:S].rearrange("p t (c i) -> p c t i", i=4))
+        z_c, z_s = quantize(z_g[:].rearrange("p c t -> p (c t)"), "z")
+
+        out_rows = out.rearrange("(p t) c -> t p c", t=PACK)
+        neg = []
+        for t in range(PACK):
+            s_bank = product(cand_w, cand_b, z_c, z_s, t, f"a{t}")
+            s_win = keep.tile([P, WIN], F32, name=f"s_win{t}")
+            nc.scalar.activation(s_win[:, 0:S], s_bank[:], ACT.Copy, scale=0.03125)
+            s_plain = keep.tile([P, S], F32, name=f"s_plain{t}")
+            nc.scalar.activation(s_plain[:], s_bank[:], ACT.Copy, scale=0.03125)
+            n_win = keep.tile([P, WIN], F32, name=f"n_win{t}")
+            nc.vector.tensor_tensor(n_win[:, 0:S], s_win[:].indirect(l_n3[:]), s_plain[:], ALU.subtract)
+            neg.append(n_win)
+        for t in range(PACK):
+            twice = keep.tile([P, S], F32, name=f"twice{t}")
+            nc.scalar.activation(twice[:], neg[t][:, 0:S], ACT.Copy, scale=2.0)
+            res = keep.tile([P, S], F32, name=f"res{t}")
+            nc.vector.tensor_tensor(res[:], neg[t][:].indirect(l_n3[:]), twice[:], ALU.subtract)
+            nc.sync.dma_start(out_rows[t], res[:])

@@ -18,7 +18,7 @@ ACT = mybir.ActivationFunctionType
 P = 128
 PACK = 4
 WIN = 2 * S
-CHUNKS = 2
+HALF = S // 2
 
 
 def tile_picked_twcgatebtwice_none_p_kernel(tc, x_words, x_scales, w1, w2, gs, offs, two, n1, n2, cand, n3, out):
@@ -32,35 +32,34 @@ def tile_picked_twcgatebtwice_none_p_kernel(tc, x_words, x_scales, w1, w2, gs, o
             nc.sync.dma_start(tile[:], src)
             return tile
 
-        xs = keep.tile([P, T], U8, name="xs", align_bytes=64)
         warm = keep.tile([P, 2], F32, name="warm")
         nc.gpsimd.memset(warm[:, 0:1], 0.0)
         nc.scalar.activation(warm[:, 1:2], warm[:, 0:1], ACT.Sigmoid)
 
+        xs = keep.tile([P, T], U8, name="xs", align_bytes=64)
         l_two = load_list(two, "l_two")
         for q in range(4):
             nc.sync.dma_start(xs[32 * q : 32 * q + 32, :].bitcast(I32),
                               x_scales[0, 4 * q : 4 * q + 4, :].bitcast(I32).partition_broadcast(8))
         l_offs = load_list(offs, "l_offs")
-        cw = H // CHUNKS
 
         def load_w(w, name):
             rows = w.rearrange("(p j) c -> p j c", j=PACK)
             raws = []
-            for h in range(CHUNKS):
-                raw = keep.tile([P, PACK, cw], F32, name=f"{name}_raw{h}")
-                nc.sync.dma_start(raw[:], rows[:, :, h * cw : (h + 1) * cw])
+            for h in range(2):
+                raw = keep.tile([P, PACK, HALF], F32, name=f"{name}_raw{h}", tag=f"{name}_raw{h}", align_bytes=64)
+                nc.sync.dma_start(raw[:], rows[:, :, h * HALF : (h + 1) * HALF])
                 raws.append(raw)
             return raws
 
-        w2_raw = load_w(w2, "w2")
         xw = keep.tile([P, T], I32, name="xw", align_bytes=64)
         nc.sync.dma_start(xw[:], x_words[0].rearrange("p n r -> p (n r)").bitcast(I32))
+        w2_raw = load_w(w2, "w2")
         l_cand = load_list(cand, "l_cand")
+        l_n2 = load_list(n2, "l_n2")
         w1_raw = load_w(w1, "w1")
         gain = keep.tile([P, PACK], F32, name="gain")
         nc.sync.dma_start(gain[:], gs.rearrange("(p t) o -> p (t o)", t=PACK))
-        l_n2 = load_list(n2, "l_n2")
         l_n1 = load_list(n1, "l_n1")
         l_n3 = load_list(n3, "l_n3")
 
@@ -74,88 +73,136 @@ def tile_picked_twcgatebtwice_none_p_kernel(tc, x_words, x_scales, w1, w2, gs, o
             nc.vector.tensor_copy(g[:], xw[:].bitcast(U32).indirect(lst[:]))
             return g
 
-        def weave_w(raws, name, on_scalar):
-            grouped = keep.tile([P, PACK, P, PACK], BF16, name=name, align_bytes=64)
-            mw = cw // PACK
-            for h in range(CHUNKS):
+        def weave_w(raws, name, copies):
+            grouped = keep.tile([P, PACK, P, PACK], BF16, name=name, tag=name, align_bytes=64)
+            mw = HALF // PACK
+            for h in range(2):
                 dst = grouped[:, :, h * mw : (h + 1) * mw, :].rearrange("p t m j -> p m t j")
                 src = raws[h][:].rearrange("p j (m t) -> p m t j", t=PACK)
-                if on_scalar:
-                    nc.scalar.copy(dst, src)
-                else:
-                    nc.gpsimd.tensor_scalar(dst, src, 1.0, 0.0, ALU.mult, ALU.add)
+                copies[h](dst, src)
             return grouped
 
-        def quantize(src, name):
-            codes = keep.tile([P, S], U32, name=name + "_codes", align_bytes=64)
-            scales = keep.tile([P, S], U8, name=name + "_scales", align_bytes=64)
-            nc.vector.quantize_mx(out=codes[:].bitcast(FP8X4), scales=scales[:], in_=src)
-            return codes, scales
+        def quantize_w(grouped, name, pieces):
+            codes = keep.tile([P, H], U32, name=f"{name}_codes", align_bytes=64)
+            scales = keep.tile([P, H], U8, name=f"{name}_scales", align_bytes=64)
+            flat = grouped[:].rearrange("p t m j -> p (t m j)")
+            width = H // pieces
+            for h in range(pieces):
+                cols = slice(h * width, (h + 1) * width)
+                nc.vector.quantize_mx(out=codes[:, cols].bitcast(FP8X4), scales=scales[:, cols],
+                                      in_=flat[:, PACK * h * width : PACK * (h + 1) * width])
+            return [(codes[:, t * P : (t + 1) * P], scales[:, t * P : (t + 1) * P]) for t in range(PACK)]
 
-        def product(lhs, lhs_s, rhs, rhs_s, t, tag):
-            bank = psum.tile([P, S], F32, name=tag, tag=tag)
-            cols = slice(t * P, (t + 1) * P)
-            nc.tensor.matmul_mx(out=bank[:], lhsT=lhs[:, cols].bitcast(FP8X4), lhsT_scale=lhs_s[:, cols],
-                                rhs=rhs[:].bitcast(FP8X4), rhs_scale=rhs_s[:], start=True, stop=True)
+        def product(lhs, rhs, tag):
+            bank = psum.tile([P, rhs[0].shape[1]], F32, name=tag, tag=tag)
+            nc.tensor.matmul_mx(out=bank[:], lhsT=lhs[0].bitcast(FP8X4), lhsT_scale=lhs[1],
+                                rhs=rhs[0].bitcast(FP8X4), rhs_scale=rhs[1], start=True, stop=True)
             return bank
 
         two_b = gather_bytes(l_two, "two_b")
         offs_b = gather_bytes(l_offs, "offs_b")
-        cand_b0 = gather_bytes(l_cand, "cand_b0")
-        w2_g = weave_w(w2_raw, "w2_g", True)
-        w2_c, w2_s = quantize(w2_g[:].rearrange("p t m j -> p (t m j)"), "w2")
         two_w = gather_words(l_two, "two_w")
         offs_w = gather_words(l_offs, "offs_w")
-        cand_w = keep.tile([P, S], U32, name="cand_w", align_bytes=64)
-        nc.vector.tensor_copy(cand_w[:].rearrange("p (t s) -> p s t", t=PACK), xw[:].bitcast(U32).indirect(l_cand[:]))
+        cand_b0 = gather_bytes(l_cand, "cand_b0")
         cand_b = keep.tile([P, S], U8, name="cand_b", align_bytes=64)
-        nc.vector.tensor_copy(cand_b[:].rearrange("p (t s) -> p t s", t=PACK), cand_b0[:].rearrange("p (s t) -> p t s", t=PACK))
-        w1_g = weave_w(w1_raw, "w1_g", False)
-        w1_c, w1_s = quantize(w1_g[:].rearrange("p t m j -> p (t m j)"), "w1")
+        nc.vector.tensor_copy(cand_b[:].bitcast(I32).rearrange("p (t a b) -> p t a b", t=PACK, b=2),
+                              cand_b0[:].bitcast(I32).rearrange("p (a t b) -> p t a b", t=PACK, b=2))
+        w2_g = weave_w(w2_raw, "w2_g", (nc.scalar.copy, nc.scalar.copy))
+        w2_q = quantize_w(w2_g, "w2", 1)
+        w1_g = weave_w(w1_raw, "w1_g", (nc.scalar.copy, nc.vector.tensor_copy))
+        w1_q = quantize_w(w1_g, "w1", 2)
+        cand_w = keep.tile([P, S], U32, name="cand_w", tag="w1_raw1", align_bytes=64)
+        nc.vector.tensor_copy(cand_w[:].rearrange("p (t a b) -> p a t b", t=PACK, b=8), xw[:].bitcast(U32).indirect(l_cand[:]))
         half_gain = keep.tile([P, PACK], F32, name="half_gain")
         nc.gpsimd.tensor_scalar(half_gain[:], gain[:], -0.5, 0.0, ALU.mult, ALU.add)
 
-        d_bank = [product(w2_c, w2_s, two_w, two_b, t, f"a{t}") for t in range(PACK)]
-        y_bank = [product(w1_c, w1_s, offs_w, offs_b, t, f"b{t}") for t in range(PACK)]
-
-        sig = []
-        for t in range(PACK):
-            d_win = keep.tile([P, WIN], F32, name=f"d_win{t}")
-            nc.scalar.copy(d_win[:, 0:S], d_bank[t][:])
-            sg = keep.tile([P, S], F32, name=f"sig{t}")
-            nc.scalar.activation(sg[:], d_win[:].indirect(l_n2[:]), ACT.Sigmoid)
-            sig.append(sg)
+        d_bank = [product(w2_q[t], (two_w[:], two_b[:]), f"a{t}") for t in range(PACK)]
+        y_bank = [product(w1_q[t], (offs_w[:], offs_b[:]), f"b{t}") for t in range(PACK)]
 
         z4 = keep.tile([P, PACK, S], F32, name="z4")
-        for t in range(PACK):
-            u_win = keep.tile([P, WIN], F32, name=f"u_win{t}")
-            nc.scalar.activation(u_win[:, 0:S], y_bank[t][:], ACT.Copy, scale=half_gain[:, t : t + 1])
-            a = keep.tile([P, S], F32, name=f"gated{t}")
-            nc.vector.scalar_tensor_tensor(a[:], y_bank[t][:], gain[:, t : t + 1], sig[t][:], ALU.mult, ALU.mult)
-            nc.vector.tensor_tensor(z4[:, t, :], u_win[:].indirect(l_n1[:]), a[:], ALU.add)
+        d_win = [keep.tile([P, WIN], F32, name=f"d_win{t}") for t in range(PACK)]
+        u_win = [keep.tile([P, WIN], F32, name=f"u_win{t}") for t in range(PACK)]
+        gated = [keep.tile([P, S], F32, name=f"gated{t}") for t in range(PACK)]
+        sig_last = keep.tile([P, S], F32, name="sig_last")
+        side = [d_win[1][:, S:WIN], d_win[2][:, S:WIN], d_win[3][:, S:WIN], sig_last[:]]
 
-        z_g = keep.tile([P, S, PACK], BF16, name="z_g", align_bytes=64)
-        split = 352
-        nc.vector.tensor_copy(z_g[:, 0:split, :].rearrange("p (c i) t -> p c t i", i=4),
-                              z4[:, :, 0:split].rearrange("p t (c i) -> p c t i", i=4))
-        nc.scalar.copy(z_g[:, split:S, :].rearrange("p (c i) t -> p c t i", i=4),
-                       z4[:, :, split:S].rearrange("p t (c i) -> p c t i", i=4))
-        z_c, z_s = quantize(z_g[:].rearrange("p c t -> p (c t)"), "z")
+        def span(h, pieces):
+            width = S // pieces
+            return slice(h * width, (h + 1) * width), slice(h * width // 16, (h + 1) * width // 16)
 
-        out_rows = out.rearrange("(p t) c -> t p c", t=PACK)
-        neg = []
-        for t in range(PACK):
-            s_bank = product(cand_w, cand_b, z_c, z_s, t, f"a{t}")
+        def open_d(t, func):
+            nc.scalar.activation(d_win[t][:, 0:S], d_bank[t][:], func)
+
+        def make_u(t):
+            nc.scalar.activation(u_win[t][:, 0:S], y_bank[t][:], ACT.Copy, scale=half_gain[:, t : t + 1])
+
+        def finish_z(t, h, pieces):
+            cols, lst = span(h, pieces)
+            nc.vector.tensor_tensor(z4[:, t, cols], u_win[t][:].indirect(l_n1[:, lst]), gated[t][:, cols], ALU.add)
+
+        def gate_on_scalar(t, h, pieces):
+            cols, lst = span(h, pieces)
+            nc.scalar.activation(side[t][:, cols], d_win[t][:].indirect(l_n2[:, lst]), ACT.Sigmoid)
+            nc.vector.scalar_tensor_tensor(gated[t][:, cols], y_bank[t][:, cols], gain[:, t : t + 1], side[t][:, cols], ALU.mult, ALU.mult)
+            finish_z(t, h, pieces)
+
+        open_d(0, ACT.Sigmoid)
+        open_d(1, ACT.Copy)
+        open_d(2, ACT.Copy)
+        nc.scalar.activation(side[0], y_bank[0][:], ACT.Copy, scale=gain[:, 0:1])
+        make_u(0)
+        nc.vector.tensor_tensor(gated[0][:], d_win[0][:].indirect(l_n2[:]), side[0], ALU.mult)
+        finish_z(0, 0, 1)
+        make_u(1)
+        gate_on_scalar(1, 0, 1)
+        make_u(2)
+        gate_on_scalar(2, 0, 1)
+        open_d(3, ACT.Copy)
+        make_u(3)
+        for h in range(2):
+            gate_on_scalar(3, h, 2)
+
+        z_c = keep.tile([P, S], U32, name="z_codes", align_bytes=64)
+        z_s = keep.tile([P, S], U8, name="z_scales", align_bytes=64)
+        z_g = []
+        for h, copy in enumerate((nc.scalar.copy, nc.vector.tensor_copy)):
+            g = keep.tile([P, HALF, PACK], BF16, name=f"z_g{h}", align_bytes=64)
+            copy(g[:].rearrange("p (c i) t -> p c t i", i=4), z4[:, :, h * HALF : (h + 1) * HALF].rearrange("p t (c i) -> p c t i", i=4))
+            z_g.append(g)
+        for h in range(2):
+            cols = slice(h * HALF, (h + 1) * HALF)
+            nc.vector.quantize_mx(out=z_c[:, cols].bitcast(FP8X4), scales=z_s[:, cols], in_=z_g[h][:].rearrange("p c t -> p (c t)"))
+
+        out_rows = out.rearrange("(a t b) c -> t a b c", t=PACK, b=8)
+        neg = {}
+
+        def first_hop(t):
             s_win = keep.tile([P, WIN], F32, name=f"s_win{t}")
-            nc.scalar.activation(s_win[:, 0:S], s_bank[:], ACT.Copy, scale=0.03125)
             s_plain = keep.tile([P, S], F32, name=f"s_plain{t}")
-            nc.scalar.activation(s_plain[:], s_bank[:], ACT.Copy, scale=0.03125)
+            pieces = 2 if t == 0 else 1
+            width = S // pieces
+            rows = slice(t * P, (t + 1) * P)
+            for h in range(pieces):
+                cols = slice(h * width, (h + 1) * width)
+                s_bank = product((cand_w[:, rows], cand_b[:, rows]), (z_c[:, cols], z_s[:, cols]), f"a{t}" if h == 0 else "b0")
+                nc.scalar.activation(s_win[:, cols], s_bank[:], ACT.Copy, scale=0.03125)
+                nc.scalar.activation(s_plain[:, cols], s_bank[:], ACT.Copy, scale=0.03125)
             n_win = keep.tile([P, WIN], F32, name=f"n_win{t}")
             nc.vector.tensor_tensor(n_win[:, 0:S], s_win[:].indirect(l_n3[:]), s_plain[:], ALU.subtract)
-            neg.append(n_win)
-        for t in range(PACK):
+            neg[t] = n_win
+
+        def second_hop(t):
             twice = keep.tile([P, S], F32, name=f"twice{t}")
             nc.scalar.activation(twice[:], neg[t][:, 0:S], ACT.Copy, scale=2.0)
             res = keep.tile([P, S], F32, name=f"res{t}")
-            nc.vector.tensor_tensor(res[:], neg[t][:].indirect(l_n3[:]), twice[:], ALU.subtract)
-            nc.sync.dma_start(out_rows[t], res[:])
+            pieces = 2 if t == PACK - 1 else 1
+            for h in range(pieces):
+                cols, lst = span(h, pieces)
+                nc.vector.tensor_tensor(res[:, cols], neg[t][:].indirect(l_n3[:, lst]), twice[:, cols], ALU.subtract)
+                nc.sync.dma_start(out_rows[t][:, :, cols], res[:, cols])
+
+        first_hop(0)
+        for t in range(1, PACK):
+            first_hop(t)
+            second_hop(t - 1)
+        second_hop(PACK - 1)

@@ -2,7 +2,9 @@ from contextlib import ExitStack
 
 import concourse.mybir as mybir
 
-K, T, S, H, C = 512, 2048, 512, 512, 512
+T = 2048
+H = 512
+S = 512
 FLOPS = 3 * 2 * 512 * 512 * 512
 
 F32 = mybir.dt.float32
@@ -17,192 +19,243 @@ ACT = mybir.ActivationFunctionType
 
 P = 128
 PACK = 4
-WIN = 2 * S
+GROUP = 16
+RUN = 8
 HALF = S // 2
+WINDOW = 2 * S
+LAST = PACK - 1
 
 
-def tile_picked_twcgatebtwice_none_p_kernel(tc, x_words, x_scales, w1, w2, gs, offs, two, n1, n2, cand, n3, out):
+def tile_picked_twcgatebtwice_none_p_kernel(
+    tc, x_words, x_scales, w1, w2, gs, offs, two, n1, n2, cand, n3, out
+):
     nc = tc.nc
     with ExitStack() as ctx:
         keep = ctx.enter_context(tc.tile_pool(name="keep", bufs=1))
         psum = ctx.enter_context(tc.psum_pool(name="psum", bufs=1))
 
         def load_list(src, name):
-            tile = keep.tile([P, S // 16], U16, name=name)
+            tile = keep.tile([P, S // GROUP], U16, name=name)
             nc.sync.dma_start(tile[:], src)
             return tile
 
-        warm = keep.tile([P, 2], F32, name="warm")
-        nc.gpsimd.memset(warm[:, 0:1], 0.0)
-        nc.scalar.activation(warm[:, 1:2], warm[:, 0:1], ACT.Sigmoid)
-
-        xs = keep.tile([P, T], U8, name="xs", align_bytes=64)
-        l_two = load_list(two, "l_two")
-        for q in range(4):
-            nc.sync.dma_start(xs[32 * q : 32 * q + 32, :].bitcast(I32),
-                              x_scales[0, 4 * q : 4 * q + 4, :].bitcast(I32).partition_broadcast(8))
-        l_offs = load_list(offs, "l_offs")
-
-        def load_w(w, name):
+        def load_weight(w, name):
             rows = w.rearrange("(p j) c -> p j c", j=PACK)
-            raws = []
+            halves = []
             for h in range(2):
                 raw = keep.tile([P, PACK, HALF], F32, name=f"{name}_raw{h}", tag=f"{name}_raw{h}", align_bytes=64)
                 nc.sync.dma_start(raw[:], rows[:, :, h * HALF : (h + 1) * HALF])
-                raws.append(raw)
-            return raws
+                halves.append(raw)
+            return halves
 
-        xw = keep.tile([P, T], I32, name="xw", align_bytes=64)
-        nc.sync.dma_start(xw[:], x_words[0].rearrange("p n r -> p (n r)").bitcast(I32))
-        w2_raw = load_w(w2, "w2")
-        l_cand = load_list(cand, "l_cand")
-        l_n2 = load_list(n2, "l_n2")
-        w1_raw = load_w(w1, "w1")
+        x_bytes = keep.tile([P, T], U8, name="x_bytes", align_bytes=64)
+        two_list = load_list(two, "two_list")
+        for q in range(4):
+            nc.sync.dma_start(
+                x_bytes[32 * q : 32 * q + 32, :].bitcast(I32),
+                x_scales[0, 4 * q : 4 * q + 4, :].bitcast(I32).partition_broadcast(8),
+            )
+        offs_list = load_list(offs, "offs_list")
+        w2_raw = load_weight(w2, "w2")
+        cand_list = load_list(cand, "cand_list")
+        x_packed = keep.tile([P, T], I32, name="x_packed", align_bytes=64)
+        nc.sync.dma_start(x_packed[:], x_words[0].rearrange("p n r -> p (n r)").bitcast(I32))
+        n2_list = load_list(n2, "n2_list")
+        w1_raw = load_weight(w1, "w1")
         gain = keep.tile([P, PACK], F32, name="gain")
         nc.sync.dma_start(gain[:], gs.rearrange("(p t) o -> p (t o)", t=PACK))
-        l_n1 = load_list(n1, "l_n1")
-        l_n3 = load_list(n3, "l_n3")
+        n1_list = load_list(n1, "n1_list")
+        n3_list = load_list(n3, "n3_list")
 
-        def gather_bytes(lst, name):
-            g = keep.tile([P, S], U8, name=name, align_bytes=64)
-            nc.vector.tensor_copy(g[:], xs[:].indirect(lst[:]))
-            return g
+        def gather_bytes(list_tile, name):
+            picked = keep.tile([P, S], U8, name=name, align_bytes=64)
+            nc.vector.tensor_copy(picked[:], x_bytes[:].indirect(list_tile[:]))
+            return picked
 
-        def gather_words(lst, name):
-            g = keep.tile([P, S], U32, name=name, align_bytes=64)
-            nc.vector.tensor_copy(g[:], xw[:].bitcast(U32).indirect(lst[:]))
-            return g
+        def gather_words(list_tile, name):
+            picked = keep.tile([P, S], U32, name=name, align_bytes=64)
+            nc.vector.tensor_copy(picked[:], x_packed[:].bitcast(U32).indirect(list_tile[:]))
+            return picked
 
-        def weave_w(raws, name, copies):
-            grouped = keep.tile([P, PACK, P, PACK], BF16, name=name, tag=name, align_bytes=64)
-            mw = HALF // PACK
+        def gpsimd_copy(dst, src):
+            nc.gpsimd.tensor_scalar(dst, src, 1.0, 0.0, ALU.mult, ALU.add)
+
+        def round_weight(halves, name, copies):
+            grouped = keep.tile([P, PACK, P, PACK], BF16, name=name, align_bytes=64)
+            m_half = P // 2
             for h in range(2):
-                dst = grouped[:, :, h * mw : (h + 1) * mw, :].rearrange("p t m j -> p m t j")
-                src = raws[h][:].rearrange("p j (m t) -> p m t j", t=PACK)
-                copies[h](dst, src)
+                copies[h](
+                    grouped[:, :, h * m_half : (h + 1) * m_half, :].rearrange("p t m j -> p m t j"),
+                    halves[h][:].rearrange("p j (m t) -> p m t j", t=PACK),
+                )
             return grouped
 
-        def quantize_w(grouped, name, pieces):
+        def quantize_weight(grouped, name, pieces):
             codes = keep.tile([P, H], U32, name=f"{name}_codes", align_bytes=64)
             scales = keep.tile([P, H], U8, name=f"{name}_scales", align_bytes=64)
             flat = grouped[:].rearrange("p t m j -> p (t m j)")
             width = H // pieces
             for h in range(pieces):
                 cols = slice(h * width, (h + 1) * width)
-                nc.vector.quantize_mx(out=codes[:, cols].bitcast(FP8X4), scales=scales[:, cols],
-                                      in_=flat[:, PACK * h * width : PACK * (h + 1) * width])
+                nc.vector.quantize_mx(
+                    out=codes[:, cols].bitcast(FP8X4),
+                    scales=scales[:, cols],
+                    in_=flat[:, PACK * h * width : PACK * (h + 1) * width],
+                )
             return [(codes[:, t * P : (t + 1) * P], scales[:, t * P : (t + 1) * P]) for t in range(PACK)]
 
         def product(lhs, rhs, tag):
             bank = psum.tile([P, rhs[0].shape[1]], F32, name=tag, tag=tag)
-            nc.tensor.matmul_mx(out=bank[:], lhsT=lhs[0].bitcast(FP8X4), lhsT_scale=lhs[1],
-                                rhs=rhs[0].bitcast(FP8X4), rhs_scale=rhs[1], start=True, stop=True)
+            nc.tensor.matmul_mx(
+                out=bank[:],
+                lhsT=lhs[0].bitcast(FP8X4),
+                lhsT_scale=lhs[1],
+                rhs=rhs[0].bitcast(FP8X4),
+                rhs_scale=rhs[1],
+                start=True,
+                stop=True,
+            )
             return bank
 
-        two_b = gather_bytes(l_two, "two_b")
-        offs_b = gather_bytes(l_offs, "offs_b")
-        two_w = gather_words(l_two, "two_w")
-        offs_w = gather_words(l_offs, "offs_w")
-        cand_b0 = gather_bytes(l_cand, "cand_b0")
-        cand_b = keep.tile([P, S], U8, name="cand_b", align_bytes=64)
-        nc.vector.tensor_copy(cand_b[:].bitcast(I32).rearrange("p (t a b) -> p t a b", t=PACK, b=2),
-                              cand_b0[:].bitcast(I32).rearrange("p (a t b) -> p t a b", t=PACK, b=2))
-        w2_g = weave_w(w2_raw, "w2_g", (nc.scalar.copy, nc.scalar.copy))
-        w2_q = quantize_w(w2_g, "w2", 1)
-        w1_g = weave_w(w1_raw, "w1_g", (nc.scalar.copy, nc.vector.tensor_copy))
-        w1_q = quantize_w(w1_g, "w1", 2)
-        cand_w = keep.tile([P, S], U32, name="cand_w", tag="w1_raw1", align_bytes=64)
-        nc.vector.tensor_copy(cand_w[:].rearrange("p (t a b) -> p a t b", t=PACK, b=8), xw[:].bitcast(U32).indirect(l_cand[:]))
-        half_gain = keep.tile([P, PACK], F32, name="half_gain")
-        nc.gpsimd.tensor_scalar(half_gain[:], gain[:], -0.5, 0.0, ALU.mult, ALU.add)
+        two_bytes = gather_bytes(two_list, "two_bytes")
+        offs_bytes = gather_bytes(offs_list, "offs_bytes")
+        cand_bytes_listed = gather_bytes(cand_list, "cand_bytes_listed")
+        cand_bytes = keep.tile([P, S], U8, name="cand_bytes", align_bytes=64)
+        nc.vector.tensor_copy(
+            cand_bytes[:].bitcast(I32).rearrange("p (t a b) -> p t a b", t=PACK, b=RUN // 4),
+            cand_bytes_listed[:].bitcast(I32).rearrange("p (a t b) -> p t a b", t=PACK, b=RUN // 4),
+        )
+        w2_mx = quantize_weight(round_weight(w2_raw, "w2_bf16", (nc.scalar.copy, nc.scalar.copy)), "w2", 1)
+        two_words = gather_words(two_list, "two_words")
+        offs_words = gather_words(offs_list, "offs_words")
+        w1_mx = quantize_weight(round_weight(w1_raw, "w1_bf16", (gpsimd_copy, nc.vector.tensor_copy)), "w1", 2)
+        cand_words = keep.tile([P, S], U32, name="cand_words", tag="w1_raw1", align_bytes=64)
+        nc.vector.tensor_copy(
+            cand_words[:].rearrange("p (t a b) -> p a t b", t=PACK, b=RUN),
+            x_packed[:].bitcast(U32).indirect(cand_list[:]),
+        )
+        minus_half_gain = keep.tile([P, PACK], F32, name="minus_half_gain")
+        nc.gpsimd.tensor_scalar(minus_half_gain[:], gain[:], -0.5, 0.0, ALU.mult, ALU.add)
 
-        d_bank = [product(w2_q[t], (two_w[:], two_b[:]), f"a{t}") for t in range(PACK)]
-        y_bank = [product(w1_q[t], (offs_w[:], offs_b[:]), f"b{t}") for t in range(PACK)]
+        d_bank = [product(w2_mx[t], (two_words[:], two_bytes[:]), f"a{t}") for t in range(PACK)]
+        y_bank = {t: product(w1_mx[t], (offs_words[:], offs_bytes[:]), f"b{t}") for t in (1, 0, 2, 3)}
 
-        z4 = keep.tile([P, PACK, S], F32, name="z4")
-        d_win = [keep.tile([P, WIN], F32, name=f"d_win{t}") for t in range(PACK)]
-        u_win = [keep.tile([P, WIN], F32, name=f"u_win{t}") for t in range(PACK)]
+        z = keep.tile([P, PACK, S], F32, name="z")
+        u_win = [keep.tile([P, WINDOW], F32, name=f"u_win{t}") for t in range(PACK)]
         gated = [keep.tile([P, S], F32, name=f"gated{t}") for t in range(PACK)]
-        sig_last = keep.tile([P, S], F32, name="sig_last")
-        side = [d_win[1][:, S:WIN], d_win[2][:, S:WIN], d_win[3][:, S:WIN], sig_last[:]]
+        d_win = {}
+        gate = {}
 
-        def span(h, pieces):
+        def spans(pieces):
             width = S // pieces
-            return slice(h * width, (h + 1) * width), slice(h * width // 16, (h + 1) * width // 16)
+            return [
+                (slice(h * width, (h + 1) * width), slice(h * width // GROUP, (h + 1) * width // GROUP))
+                for h in range(pieces)
+            ]
 
-        def open_d(t, func):
+        def open_d(t, tag, func):
+            d_win[t] = keep.tile([P, WINDOW], F32, name=f"d_win{t}", tag=tag)
             nc.scalar.activation(d_win[t][:, 0:S], d_bank[t][:], func)
 
-        def make_u(t):
-            nc.scalar.activation(u_win[t][:, 0:S], y_bank[t][:], ACT.Copy, scale=half_gain[:, t : t + 1])
+        def copy_u(t):
+            nc.scalar.activation(u_win[t][:, 0:S], y_bank[t][:], ACT.Copy, scale=minus_half_gain[:, t : t + 1])
 
-        def finish_z(t, h, pieces):
-            cols, lst = span(h, pieces)
-            nc.vector.tensor_tensor(z4[:, t, cols], u_win[t][:].indirect(l_n1[:, lst]), gated[t][:, cols], ALU.add)
+        def look_up_gate(t, dst, pieces=1):
+            gate[t] = dst
+            for cols, entries in spans(pieces):
+                nc.scalar.activation(gate[t][:, cols], d_win[t][:].indirect(n2_list[:, entries]), ACT.Sigmoid)
 
-        def gate_on_scalar(t, h, pieces):
-            cols, lst = span(h, pieces)
-            nc.scalar.activation(side[t][:, cols], d_win[t][:].indirect(l_n2[:, lst]), ACT.Sigmoid)
-            nc.vector.scalar_tensor_tensor(gated[t][:, cols], y_bank[t][:, cols], gain[:, t : t + 1], side[t][:, cols], ALU.mult, ALU.mult)
-            finish_z(t, h, pieces)
+        def apply_gate(t, pieces=1):
+            for cols, entries in spans(pieces):
+                nc.vector.scalar_tensor_tensor(
+                    gated[t][:, cols], y_bank[t][:, cols], gain[:, t : t + 1], gate[t][:, cols], ALU.mult, ALU.mult
+                )
 
-        open_d(0, ACT.Sigmoid)
-        open_d(1, ACT.Copy)
-        open_d(2, ACT.Copy)
-        nc.scalar.activation(side[0], y_bank[0][:], ACT.Copy, scale=gain[:, 0:1])
-        make_u(0)
-        nc.vector.tensor_tensor(gated[0][:], d_win[0][:].indirect(l_n2[:]), side[0], ALU.mult)
-        finish_z(0, 0, 1)
-        make_u(1)
-        gate_on_scalar(1, 0, 1)
-        make_u(2)
-        gate_on_scalar(2, 0, 1)
-        open_d(3, ACT.Copy)
-        make_u(3)
-        for h in range(2):
-            gate_on_scalar(3, h, 2)
+        def finish_z(t, pieces=1):
+            for cols, entries in spans(pieces):
+                nc.vector.tensor_tensor(
+                    z[:, t, cols], u_win[t][:].indirect(n1_list[:, entries]), gated[t][:, cols], ALU.add
+                )
 
-        z_c = keep.tile([P, S], U32, name="z_codes", align_bytes=64)
-        z_s = keep.tile([P, S], U8, name="z_scales", align_bytes=64)
-        z_g = []
+        open_d(0, "d_win0", ACT.Sigmoid)
+        open_d(1, "d_win1", ACT.Copy)
+        gate_1 = keep.tile([P, S], F32, name="gate_1")
+        look_up_gate(1, gate_1[:])
+        open_d(2, "d_win2", ACT.Copy)
+        apply_gate(1)
+        y_gain = d_win[2][:, S:WINDOW]
+        nc.scalar.activation(y_gain, y_bank[0][:], ACT.Copy, scale=gain[:, 0:1])
+        copy_u(1)
+        copy_u(0)
+        nc.vector.tensor_tensor(gated[0][:], d_win[0][:].indirect(n2_list[:]), y_gain, ALU.mult)
+        finish_z(1)
+        finish_z(0)
+        copy_u(2)
+        d_last = keep.tile([P, WINDOW], F32, name="d_win3", tag="d_win0")
+        look_up_gate(2, d_last[:, S:WINDOW])
+        apply_gate(2)
+        finish_z(2)
+        d_win[LAST] = d_last
+        nc.scalar.activation(d_last[:, 0:S], d_bank[LAST][:], ACT.Copy)
+        copy_u(LAST)
+        gate_last = keep.tile([P, S], F32, name="gate_last")
+        look_up_gate(LAST, gate_last[:], 2)
+        apply_gate(LAST, 2)
+        finish_z(LAST, 2)
+
+        z_codes = keep.tile([P, S], U32, name="z_codes", align_bytes=64)
+        z_scales = keep.tile([P, S], U8, name="z_scales", align_bytes=64)
+        z_bf16 = []
         for h, copy in enumerate((nc.scalar.copy, nc.vector.tensor_copy)):
-            g = keep.tile([P, HALF, PACK], BF16, name=f"z_g{h}", align_bytes=64)
-            copy(g[:].rearrange("p (c i) t -> p c t i", i=4), z4[:, :, h * HALF : (h + 1) * HALF].rearrange("p t (c i) -> p c t i", i=4))
-            z_g.append(g)
+            grouped = keep.tile([P, HALF, PACK], BF16, name=f"z_bf16_{h}", align_bytes=64)
+            copy(
+                grouped[:].rearrange("p (c i) t -> p c t i", i=4),
+                z[:, :, h * HALF : (h + 1) * HALF].rearrange("p t (c i) -> p c t i", i=4),
+            )
+            z_bf16.append(grouped)
         for h in range(2):
             cols = slice(h * HALF, (h + 1) * HALF)
-            nc.vector.quantize_mx(out=z_c[:, cols].bitcast(FP8X4), scales=z_s[:, cols], in_=z_g[h][:].rearrange("p c t -> p (c t)"))
+            nc.vector.quantize_mx(
+                out=z_codes[:, cols].bitcast(FP8X4),
+                scales=z_scales[:, cols],
+                in_=z_bf16[h][:].rearrange("p c t -> p (c t)"),
+            )
 
-        out_rows = out.rearrange("(a t b) c -> t a b c", t=PACK, b=8)
-        neg = {}
+        half_of_sixteenth = 0.03125
+        out_rows = out.rearrange("(a t b) c -> t a b c", t=PACK, b=RUN)
+        g_win = {}
 
         def first_hop(t):
-            s_win = keep.tile([P, WIN], F32, name=f"s_win{t}")
-            s_plain = keep.tile([P, S], F32, name=f"s_plain{t}")
-            pieces = 2 if t == 0 else 1
-            width = S // pieces
+            h_win = keep.tile([P, WINDOW], F32, name=f"h_win{t}")
+            h_plain = keep.tile([P, S], F32, name=f"h_plain{t}")
             rows = slice(t * P, (t + 1) * P)
-            for h in range(pieces):
-                cols = slice(h * width, (h + 1) * width)
-                s_bank = product((cand_w[:, rows], cand_b[:, rows]), (z_c[:, cols], z_s[:, cols]), f"a{t}" if h == 0 else "b0")
-                nc.scalar.activation(s_win[:, cols], s_bank[:], ACT.Copy, scale=0.03125)
-                nc.scalar.activation(s_plain[:, cols], s_bank[:], ACT.Copy, scale=0.03125)
-            n_win = keep.tile([P, WIN], F32, name=f"n_win{t}")
-            nc.vector.tensor_tensor(n_win[:, 0:S], s_win[:].indirect(l_n3[:]), s_plain[:], ALU.subtract)
-            neg[t] = n_win
+            lhs = (cand_words[:, rows], cand_bytes[:, rows])
+            pieces = spans(2 if t == 0 else 1)
+            for h, (cols, entries) in enumerate(pieces):
+                s_bank = product(lhs, (z_codes[:, cols], z_scales[:, cols]), f"a{t}" if h == 0 else "b0")
+                nc.scalar.activation(h_win[:, cols], s_bank[:], ACT.Copy, scale=half_of_sixteenth)
+                if t == 0 and h == 0:
+                    nc.vector.tensor_scalar(h_plain[:, cols], s_bank[:], half_of_sixteenth, None, ALU.mult)
+                else:
+                    nc.scalar.activation(h_plain[:, cols], s_bank[:], ACT.Copy, scale=half_of_sixteenth)
+            g_win[t] = keep.tile([P, WINDOW], F32, name=f"g_win{t}")
+            for cols, entries in pieces:
+                nc.vector.tensor_tensor(
+                    g_win[t][:, cols], h_win[:].indirect(n3_list[:, entries]), h_plain[:, cols], ALU.subtract
+                )
 
         def second_hop(t):
-            twice = keep.tile([P, S], F32, name=f"twice{t}")
-            nc.scalar.activation(twice[:], neg[t][:, 0:S], ACT.Copy, scale=2.0)
-            res = keep.tile([P, S], F32, name=f"res{t}")
-            pieces = 2 if t == PACK - 1 else 1
-            for h in range(pieces):
-                cols, lst = span(h, pieces)
-                nc.vector.tensor_tensor(res[:, cols], neg[t][:].indirect(l_n3[:, lst]), twice[:, cols], ALU.subtract)
-                nc.sync.dma_start(out_rows[t][:, :, cols], res[:, cols])
+            twice_g = keep.tile([P, S], F32, name=f"twice_g{t}")
+            nc.scalar.activation(twice_g[:], g_win[t][:, 0:S], ACT.Copy, scale=2.0)
+            result = keep.tile([P, S], F32, name=f"result{t}")
+            for cols, entries in spans(2 if t == LAST else 1):
+                nc.vector.tensor_tensor(
+                    result[:, cols], g_win[t][:].indirect(n3_list[:, entries]), twice_g[:, cols], ALU.subtract
+                )
+                nc.sync.dma_start(out_rows[t][:, :, cols], result[:, cols])
 
         first_hop(0)
         for t in range(1, PACK):
             first_hop(t)
             second_hop(t - 1)
-        second_hop(PACK - 1)
+        second_hop(LAST)

from contextlib import ExitStack

import concourse.mybir as mybir

T = 2048
H = 512
S = 512
FLOPS = 3 * 2 * 512 * 512 * 512

F32 = mybir.dt.float32
BF16 = mybir.dt.bfloat16
I32 = mybir.dt.int32
U32 = mybir.dt.uint32
U16 = mybir.dt.uint16
U8 = mybir.dt.uint8
FP8X4 = mybir.dt.float8_e4m3fn_x4
ALU = mybir.AluOpType
ACT = mybir.ActivationFunctionType

P = 128
PACK = 4
GROUP = 16
RUN = 8
HALF = S // 2
WINDOW = 2 * S
LAST = PACK - 1


def tile_picked_twcgatebtwice_none_p_kernel(
    tc, x_words, x_scales, w1, w2, gs, offs, two, n1, n2, cand, n3, out
):
    nc = tc.nc
    with ExitStack() as ctx:
        keep = ctx.enter_context(tc.tile_pool(name="keep", bufs=1))
        psum = ctx.enter_context(tc.psum_pool(name="psum", bufs=1))

        def load_list(src, name):
            tile = keep.tile([P, S // GROUP], U16, name=name)
            nc.sync.dma_start(tile[:], src)
            return tile

        def load_weight(w, name):
            rows = w.rearrange("(p j) c -> p j c", j=PACK)
            halves = []
            for h in range(2):
                raw = keep.tile([P, PACK, HALF], F32, name=f"{name}_raw{h}", tag=f"{name}_raw{h}", align_bytes=64)
                nc.sync.dma_start(raw[:], rows[:, :, h * HALF : (h + 1) * HALF])
                halves.append(raw)
            return halves

        x_bytes = keep.tile([P, T], U8, name="x_bytes", align_bytes=64)
        two_list = load_list(two, "two_list")
        for q in range(4):
            nc.sync.dma_start(
                x_bytes[32 * q : 32 * q + 32, :].bitcast(I32),
                x_scales[0, 4 * q : 4 * q + 4, :].bitcast(I32).partition_broadcast(8),
            )
        offs_list = load_list(offs, "offs_list")
        w2_raw = load_weight(w2, "w2")
        cand_list = load_list(cand, "cand_list")
        x_packed = keep.tile([P, T], I32, name="x_packed", align_bytes=64)
        nc.sync.dma_start(x_packed[:], x_words[0].rearrange("p n r -> p (n r)").bitcast(I32))
        n2_list = load_list(n2, "n2_list")
        w1_raw = load_weight(w1, "w1")
        gain = keep.tile([P, PACK], F32, name="gain")
        nc.sync.dma_start(gain[:], gs.rearrange("(p t) o -> p (t o)", t=PACK))
        n1_list = load_list(n1, "n1_list")
        n3_list = load_list(n3, "n3_list")

        def gather_bytes(list_tile, name):
            picked = keep.tile([P, S], U8, name=name, align_bytes=64)
            nc.vector.tensor_copy(picked[:], x_bytes[:].indirect(list_tile[:]))
            return picked

        def gather_words(list_tile, name):
            picked = keep.tile([P, S], U32, name=name, align_bytes=64)
            nc.vector.tensor_copy(picked[:], x_packed[:].bitcast(U32).indirect(list_tile[:]))
            return picked

        def gpsimd_copy(dst, src):
            nc.gpsimd.tensor_scalar(dst, src, 1.0, 0.0, ALU.mult, ALU.add)

        def round_weight(halves, name, copies):
            grouped = keep.tile([P, PACK, P, PACK], BF16, name=name, align_bytes=64)
            m_half = P // 2
            for h in range(2):
                copies[h](
                    grouped[:, :, h * m_half : (h + 1) * m_half, :].rearrange("p t m j -> p m t j"),
                    halves[h][:].rearrange("p j (m t) -> p m t j", t=PACK),
                )
            return grouped

        def quantize_weight(grouped, name, pieces):
            codes = keep.tile([P, H], U32, name=f"{name}_codes", align_bytes=64)
            scales = keep.tile([P, H], U8, name=f"{name}_scales", align_bytes=64)
            flat = grouped[:].rearrange("p t m j -> p (t m j)")
            width = H // pieces
            for h in range(pieces):
                cols = slice(h * width, (h + 1) * width)
                nc.vector.quantize_mx(
                    out=codes[:, cols].bitcast(FP8X4),
                    scales=scales[:, cols],
                    in_=flat[:, PACK * h * width : PACK * (h + 1) * width],
                )
            return [(codes[:, t * P : (t + 1) * P], scales[:, t * P : (t + 1) * P]) for t in range(PACK)]

        def product(lhs, rhs, tag):
            bank = psum.tile([P, rhs[0].shape[1]], F32, name=tag, tag=tag)
            nc.tensor.matmul_mx(
                out=bank[:],
                lhsT=lhs[0].bitcast(FP8X4),
                lhsT_scale=lhs[1],
                rhs=rhs[0].bitcast(FP8X4),
                rhs_scale=rhs[1],
                start=True,
                stop=True,
            )
            return bank

        two_bytes = gather_bytes(two_list, "two_bytes")
        offs_bytes = gather_bytes(offs_list, "offs_bytes")
        cand_bytes_listed = gather_bytes(cand_list, "cand_bytes_listed")
        cand_bytes = keep.tile([P, S], U8, name="cand_bytes", align_bytes=64)
        nc.vector.tensor_copy(
            cand_bytes[:].bitcast(I32).rearrange("p (t a b) -> p t a b", t=PACK, b=RUN // 4),
            cand_bytes_listed[:].bitcast(I32).rearrange("p (a t b) -> p t a b", t=PACK, b=RUN // 4),
        )
        w2_mx = quantize_weight(round_weight(w2_raw, "w2_bf16", (nc.scalar.copy, nc.scalar.copy)), "w2", 1)
        two_words = gather_words(two_list, "two_words")
        offs_words = gather_words(offs_list, "offs_words")
        w1_mx = quantize_weight(round_weight(w1_raw, "w1_bf16", (gpsimd_copy, nc.vector.tensor_copy)), "w1", 2)
        cand_words = keep.tile([P, S], U32, name="cand_words", tag="w1_raw1", align_bytes=64)
        nc.vector.tensor_copy(
            cand_words[:].rearrange("p (t a b) -> p a t b", t=PACK, b=RUN),
            x_packed[:].bitcast(U32).indirect(cand_list[:]),
        )
        minus_half_gain = keep.tile([P, PACK], F32, name="minus_half_gain")
        nc.gpsimd.tensor_scalar(minus_half_gain[:], gain[:], -0.5, 0.0, ALU.mult, ALU.add)

        d_bank = [product(w2_mx[t], (two_words[:], two_bytes[:]), f"a{t}") for t in range(PACK)]
        y_bank = {t: product(w1_mx[t], (offs_words[:], offs_bytes[:]), f"b{t}") for t in (1, 0, 2, 3)}

        z = keep.tile([P, PACK, S], F32, name="z")
        u_win = [keep.tile([P, WINDOW], F32, name=f"u_win{t}") for t in range(PACK)]
        gated = [keep.tile([P, S], F32, name=f"gated{t}") for t in range(PACK)]
        d_win = {}
        gate = {}

        def spans(pieces):
            width = S // pieces
            return [
                (slice(h * width, (h + 1) * width), slice(h * width // GROUP, (h + 1) * width // GROUP))
                for h in range(pieces)
            ]

        def open_d(t, tag, func):
            d_win[t] = keep.tile([P, WINDOW], F32, name=f"d_win{t}", tag=tag)
            nc.scalar.activation(d_win[t][:, 0:S], d_bank[t][:], func)

        def copy_u(t):
            nc.scalar.activation(u_win[t][:, 0:S], y_bank[t][:], ACT.Copy, scale=minus_half_gain[:, t : t + 1])

        def look_up_gate(t, dst, pieces=1):
            gate[t] = dst
            for cols, entries in spans(pieces):
                nc.scalar.activation(gate[t][:, cols], d_win[t][:].indirect(n2_list[:, entries]), ACT.Sigmoid)

        def apply_gate(t, pieces=1):
            for cols, entries in spans(pieces):
                nc.vector.scalar_tensor_tensor(
                    gated[t][:, cols], y_bank[t][:, cols], gain[:, t : t + 1], gate[t][:, cols], ALU.mult, ALU.mult
                )

        def finish_z(t, pieces=1):
            for cols, entries in spans(pieces):
                nc.vector.tensor_tensor(
                    z[:, t, cols], u_win[t][:].indirect(n1_list[:, entries]), gated[t][:, cols], ALU.add
                )

        open_d(0, "d_win0", ACT.Sigmoid)
        open_d(1, "d_win1", ACT.Copy)
        gate_1 = keep.tile([P, S], F32, name="gate_1")
        look_up_gate(1, gate_1[:])
        open_d(2, "d_win2", ACT.Copy)
        apply_gate(1)
        y_gain = d_win[2][:, S:WINDOW]
        nc.scalar.activation(y_gain, y_bank[0][:], ACT.Copy, scale=gain[:, 0:1])
        copy_u(1)
        copy_u(0)
        nc.vector.tensor_tensor(gated[0][:], d_win[0][:].indirect(n2_list[:]), y_gain, ALU.mult)
        finish_z(1)
        finish_z(0)
        copy_u(2)
        d_last = keep.tile([P, WINDOW], F32, name="d_win3", tag="d_win0")
        look_up_gate(2, d_last[:, S:WINDOW])
        apply_gate(2)
        finish_z(2)
        d_win[LAST] = d_last
        nc.scalar.activation(d_last[:, 0:S], d_bank[LAST][:], ACT.Copy)
        copy_u(LAST)
        gate_last = keep.tile([P, S], F32, name="gate_last")
        look_up_gate(LAST, gate_last[:], 2)
        apply_gate(LAST, 2)
        finish_z(LAST, 2)

        z_codes = keep.tile([P, S], U32, name="z_codes", align_bytes=64)
        z_scales = keep.tile([P, S], U8, name="z_scales", align_bytes=64)
        z_bf16 = []
        for h, copy in enumerate((nc.scalar.copy, nc.vector.tensor_copy)):
            grouped = keep.tile([P, HALF, PACK], BF16, name=f"z_bf16_{h}", align_bytes=64)
            copy(
                grouped[:].rearrange("p (c i) t -> p c t i", i=4),
                z[:, :, h * HALF : (h + 1) * HALF].rearrange("p t (c i) -> p c t i", i=4),
            )
            z_bf16.append(grouped)
        for h in range(2):
            cols = slice(h * HALF, (h + 1) * HALF)
            nc.vector.quantize_mx(
                out=z_codes[:, cols].bitcast(FP8X4),
                scales=z_scales[:, cols],
                in_=z_bf16[h][:].rearrange("p c t -> p (c t)"),
            )

        half_of_sixteenth = 0.03125
        out_rows = out.rearrange("(a t b) c -> t a b c", t=PACK, b=RUN)
        g_win = {}

        def first_hop(t):
            h_win = keep.tile([P, WINDOW], F32, name=f"h_win{t}")
            h_plain = keep.tile([P, S], F32, name=f"h_plain{t}")
            rows = slice(t * P, (t + 1) * P)
            lhs = (cand_words[:, rows], cand_bytes[:, rows])
            pieces = spans(2 if t == 0 else 1)
            for h, (cols, entries) in enumerate(pieces):
                s_bank = product(lhs, (z_codes[:, cols], z_scales[:, cols]), f"a{t}" if h == 0 else "b0")
                nc.scalar.activation(h_win[:, cols], s_bank[:], ACT.Copy, scale=half_of_sixteenth)
                if t == 0 and h == 0:
                    nc.vector.tensor_scalar(h_plain[:, cols], s_bank[:], half_of_sixteenth, None, ALU.mult)
                else:
                    nc.scalar.activation(h_plain[:, cols], s_bank[:], ACT.Copy, scale=half_of_sixteenth)
            g_win[t] = keep.tile([P, WINDOW], F32, name=f"g_win{t}")
            for cols, entries in pieces:
                nc.vector.tensor_tensor(
                    g_win[t][:, cols], h_win[:].indirect(n3_list[:, entries]), h_plain[:, cols], ALU.subtract
                )

        def second_hop(t):
            twice_g = keep.tile([P, S], F32, name=f"twice_g{t}")
            nc.scalar.activation(twice_g[:], g_win[t][:, 0:S], ACT.Copy, scale=2.0)
            result = keep.tile([P, S], F32, name=f"result{t}")
            for cols, entries in spans(2 if t == LAST else 1):
                nc.vector.tensor_tensor(
                    result[:, cols], g_win[t][:].indirect(n3_list[:, entries]), twice_g[:, cols], ALU.subtract
                )
                nc.sync.dma_start(out_rows[t][:, :, cols], result[:, cols])

        first_hop(0)
        for t in range(1, PACK):
            first_hop(t)
            second_hop(t - 1)
        second_hop(LAST)
